import numpy as np
import ml_dtypes


def mxq(x, axis, fmt="e4m3"):
    dtype, down = {"e4m3": (ml_dtypes.float8_e4m3fn, 7), "e5m2": (ml_dtypes.float8_e5m2, 14)}[fmt]
    v = np.moveaxis(np.asarray(x, np.float32).astype(ml_dtypes.bfloat16).astype(np.float64), axis, -1)
    blocks = v.reshape(v.shape[:-1] + (-1, 32))
    amax = np.abs(blocks).max(-1, keepdims=True)
    byte = np.maximum(np.where(amax > 0, np.frexp(amax)[1] - 1 + 127, 0) - down, 1)
    scale = np.exp2(byte - 127.0)
    codes = (blocks / scale).astype(np.float32).astype(dtype).astype(np.float64)
    return np.moveaxis((codes * scale).reshape(v.shape), -1, axis)


WIDE = False


def mx_kscale(k):
    if not WIDE:
        return np.ones(k)
    levels = np.array([10, -10, 5, -5, 0])
    if k % 512:
        return np.exp2(np.random.permutation(np.resize(levels, k // 32))).repeat(32)
    a = np.empty((k // 512, 16))
    for p in range(k // 512):
        a[p, :8] = np.random.permutation(np.resize(levels, 8))
        for g in range(8):
            far = levels[np.abs(levels - a[p, g]) >= 10]
            a[p, g + 8] = far[np.random.randint(len(far))]
    return np.exp2(a.ravel()).repeat(32)


def f64(x):
    return np.asarray(x).astype(np.float64)


def striped(idx):
    return np.tile(idx.reshape(-1, 16).T, (8, 1)).astype(np.uint16)


def unstriped(offs):
    return offs[:16].T.reshape(-1).astype(np.int64)


def striped8(idx):
    return np.concatenate([x.reshape(-1, 16).T for x in idx]).astype(np.uint16)


def runs(offs, k):
    lists = np.stack([offs[16 * r : 16 * r + 16].T.reshape(-1) for r in range(8)]).astype(np.int64)
    return lists[np.arange(k) % 512 // 64]


def pack_weight(w):
    k, n = w.shape
    w = f64(np.asarray(w, np.float32).astype(ml_dtypes.bfloat16)).reshape(k // 32, 32, n)
    amax = np.abs(w).max(1)
    byte = np.clip(np.where(amax > 0, np.frexp(amax)[1] - 1 + 127 - 7, 1), 1, 254)
    scaled = (w * np.exp2(127.0 - byte)[:, None, :]).reshape(k, n).astype(np.float32)
    words = np.ascontiguousarray(scaled.reshape(k // 512, 128, 4, n).transpose(0, 1, 3, 2)).astype(ml_dtypes.float8_e4m3fn).view(np.uint8)
    return words, np.ascontiguousarray(byte.astype(np.uint8).reshape(k // 512, 16, n))


def unpack_weight(words, scales):
    g, p, n, _ = words.shape
    vals = np.ascontiguousarray(words).view(ml_dtypes.float8_e4m3fn).astype(np.float64) * np.repeat(np.exp2(scales.astype(np.float64) - 127.0), 8, axis=1)[..., None]
    return vals.transpose(0, 1, 3, 2).reshape(g * 512, n)


E2M1 = np.array([0.0, 0.5, 1.0, 1.5, 2.0, 3.0, 4.0, 6.0, -0.0, -0.5, -1.0, -1.5, -2.0, -3.0, -4.0, -6.0])


def pack_fp4(w):
    k, n = w.shape
    w = f64(np.asarray(w, np.float32).astype(ml_dtypes.bfloat16)).reshape(k // 32, 32, n)
    amax = np.abs(w).max(1)
    mant, ex = np.frexp(amax / 6.0)
    byte = np.clip(np.where(amax > 0, np.where(mant > 0.5, ex, ex - 1) + 127, 1), 1, 254)
    scaled = (w * np.exp2(127.0 - byte)[:, None, :]).reshape(k, n).astype(np.float32)
    c = np.ascontiguousarray(scaled.reshape(k // 512, 128, 4, n).transpose(0, 1, 3, 2)).astype(ml_dtypes.float4_e2m1fn).view(np.uint8) & 0xF
    words = (c[..., 0::2] | (c[..., 1::2] << 4)).reshape(k // 512, 128, 2 * n)
    return np.ascontiguousarray(words), np.ascontiguousarray(byte.astype(np.uint8).reshape(k // 512, 16, n))


def unpack_fp4(words, scales):
    g, _, n = scales.shape
    words = np.ascontiguousarray(words).reshape(g, 128, n, 2)
    nib = np.empty((g, 128, n, 4), np.uint8)
    nib[..., 0::2] = words & 0xF
    nib[..., 1::2] = words >> 4
    vals = E2M1[nib] * np.repeat(np.exp2(scales.astype(np.float64) - 127.0), 8, axis=1)[..., None]
    return vals.transpose(0, 1, 3, 2).reshape(g * 512, n)


def planes(y):
    n, m = y.shape
    v = y.astype(np.float32).astype(ml_dtypes.bfloat16).astype(np.float64).reshape(n // 32, 32, m)
    top = np.abs(v).max(1)
    byte = np.clip(np.where(top > 0, np.frexp(top)[1] - 1 + 127 - 7, 1), 1, 254)
    codes = (v * np.exp2(127.0 - byte)[:, None, :]).reshape(n, m).astype(np.float32).astype(ml_dtypes.float8_e4m3fn).view(np.uint8)
    words = codes.reshape(n // 512, 128, 4, m).transpose(0, 1, 3, 2)
    return np.ascontiguousarray(words), np.ascontiguousarray(byte.astype(np.uint8).reshape(n // 512, 16, m))


K, T, S, H, J = 512, 2048, 512, 512, 512


def setup_inputs():
    n = np.random.standard_normal
    s = mx_kscale(K)[:, None]
    u = mx_kscale(H)
    packed_xT = pack_weight(n((K, T)) * s)
    packed_w1 = pack_fp4(n((K, H)) / np.sqrt(K) / s)
    packed_w2 = pack_fp4(n((H, H)) / np.sqrt(H) / u[:, None])
    return {
        "x_words": packed_xT[0],
        "x_scales": packed_xT[1],
        "w1_words": packed_w1[0],
        "w1_scales": packed_w1[1],
        "tab": n((H, J)).astype(np.float32),
        "gn": (np.random.uniform(0.5, 1.5, (H, 1)) * u[:, None]).astype(np.float32),
        "w2_words": packed_w2[0],
        "w2_scales": packed_w2[1],
        "offs": striped(np.random.permutation(T)[:S]),
        "n1": striped8(np.stack([np.random.permutation(S) for _ in range(8)])),
        "n2": striped8(np.stack([np.random.permutation(S) for _ in range(8)])),
        "n3": striped8(np.stack([np.random.permutation(S) for _ in range(8)])),
        "n4": striped8(np.random.randint(0, J, (8, S))),
        "n5": striped8(np.random.randint(0, J, (8, S))),
        "n6": striped8(np.stack([np.random.permutation(S) for _ in range(8)])),
        "n7": striped8(np.stack([np.random.permutation(S) for _ in range(8)])),
        "n8": striped8(np.stack([np.random.permutation(S) for _ in range(8)])),
    }


def reference(x_words, x_scales, w1_words, w1_scales, tab, gn, w2_words, w2_scales, offs, n1, n2, n3, n4, n5, n6, n7, n8):
    xq = unpack_weight(x_words, x_scales)[:, unstriped(offs)]
    y = unpack_fp4(w1_words, w1_scales).T @ xq
    z = f64(gn) * (y + y[np.arange(H)[:, None], runs(n1, H)] - (np.maximum(y[np.arange(H)[:, None], runs(n2, H)], y[np.arange(H)[:, None], runs(n3, H)])))
    w2q = unpack_fp4(w2_words, w2_scales)
    a = w2q.T @ mxq(z, 0, "e4m3")
    z2 = f64(gn) * ((y[np.arange(H)[:, None], runs(n6, H)]) * (f64(tab)[np.arange(H)[:, None], runs(n4, H)]) + f64(tab)[np.arange(H)[:, None], runs(n5, H)])
    b = w2q.T @ mxq(z2, 0, "e4m3")
    out_0 = (a - (a[np.arange(H)[:, None], runs(n7, H)])) / (np.abs(b) + np.abs(b[np.arange(H)[:, None], runs(n8, H)]) + 0.5)
    return (out_0,) + planes(out_0)

@@ -1,0 +1,234 @@
+from contextlib import ExitStack
+
+import concourse.mybir as mybir
+
+K, T, S, H = 512, 2048, 512, 512
+FLOPS = 3 * 2 * K * H * S
+
+F32 = mybir.dt.float32
+BF16 = mybir.dt.bfloat16
+I32 = mybir.dt.int32
+U32 = mybir.dt.uint32
+U16 = mybir.dt.uint16
+U8 = mybir.dt.uint8
+FP8X4 = mybir.dt.float8_e4m3fn_x4
+FP4X4 = mybir.dt.float4_e2m1fn_x4
+ALU = mybir.AluOpType
+ACT = mybir.ActivationFunctionType
+
+P = 128
+PACK = 4
+HALF = S // 2
+LANES = 16
+
+
+def tile_picked_tienormbtrimkinda_none_po_kernel(
+    tc, x_words, x_scales, w1_words, w1_scales, tab, gn, w2_words, w2_scales,
+    offs, n1, n2, n3, n4, n5, n6, n7, n8, out_0, out_1, out_2,
+):
+    nc = tc.nc
+    with ExitStack() as ctx:
+        keep = ctx.enter_context(tc.tile_pool(name="keep", bufs=1))
+        psum = ctx.enter_context(tc.psum_pool(name="psum", bufs=1))
+
+        def load_list(name, src):
+            tile = keep.tile([P, S // LANES], U16, name=name)
+            nc.sync.dma_start(tile[:], src)
+            return tile
+
+        def entries(tile, first, count):
+            return tile[:, first // LANES : (first + count) // LANES]
+
+        def load_scale_rows(queue, clear, name, src, width):
+            tile = keep.tile([P, width], U8, name=name, align_bytes=64)
+            clear.memset(tile[:].bitcast(I32), 0)
+            for q in range(4):
+                queue.dma_start(tile[32 * q : 32 * q + 4, :].bitcast(I32), src[0, 4 * q : 4 * q + 4, :].bitcast(I32))
+            return tile
+
+        def deal(name, words_raw, scales_raw):
+            words = keep.tile([P, 2 * H], U8, name=name + "_words", align_bytes=64)
+            scales = keep.tile([P, H], U8, name=name + "_scales", align_bytes=64)
+            nc.vector.tensor_copy(
+                words[:].rearrange("p (t m b) -> p t m b", t=PACK, b=2),
+                words_raw[:].rearrange("p (m t b) -> p t m b", t=PACK, b=2),
+            )
+            nc.vector.tensor_copy(
+                scales[:].rearrange("p (t m) -> p t m", t=PACK),
+                scales_raw[:].rearrange("p (m t) -> p t m", t=PACK),
+            )
+            return words, scales
+
+        def product(out, weights, t, codes, scales):
+            words, w_scales = weights
+            nc.tensor.matmul_mx(
+                out=out,
+                lhsT=words[:, 2 * P * t : 2 * P * (t + 1)].bitcast(FP4X4),
+                lhsT_scale=w_scales[:, P * t : P * (t + 1)],
+                rhs=codes.bitcast(FP8X4),
+                rhs_scale=scales,
+                start=True,
+                stop=True,
+            )
+
+        w1s_raw = load_scale_rows(nc.scalar, nc.gpsimd, "w1s_raw", w1_scales, H)
+        xs = load_scale_rows(nc.scalar, nc.gpsimd, "xs", x_scales, T)
+        w2s_raw = load_scale_rows(nc.gpsimd, nc.gpsimd, "w2s_raw", w2_scales, H)
+
+        tab_rows = tab.rearrange("(p t) j -> p t j", t=PACK)
+        tab_raw = [keep.tile([P, 2, S], F32, name="tab_raw%d" % u) for u in range(2)]
+        tabw = [keep.tile([P, 2 * S], F32, name="tabw%d" % t) for t in range(PACK)]
+        gain = keep.tile([P, PACK], F32, name="gain")
+        xw = keep.tile([P, T], U32, name="xw")
+        w1w_raw = keep.tile([P, 2 * H], U8, name="w1w_raw")
+        w2w_raw = keep.tile([P, 2 * H], U8, name="w2w_raw")
+
+        nc.sync.dma_start(w1w_raw[:].bitcast(I32), w1_words[0].bitcast(I32))
+        nc.sync.dma_start(w2w_raw[:].bitcast(I32), w2_words[0].bitcast(I32))
+        nc.sync.dma_start(xw[:].bitcast(I32), x_words[0].rearrange("p c r -> p (c r)").bitcast(I32))
+        picks = load_list("picks", offs)
+        nc.sync.dma_start(gain[:], gn.rearrange("(p t) o -> p (t o)", t=PACK))
+        nc.sync.dma_start(tab_raw[0][:], tab_rows[:, 0:2, :])
+        l4 = load_list("l4", n4)
+        nc.sync.dma_start(tab_raw[1][:], tab_rows[:, 2:4, :])
+        l6 = load_list("l6", n6)
+        l5 = load_list("l5", n5)
+        l1 = load_list("l1", n1)
+        l2 = load_list("l2", n2)
+        l3 = load_list("l3", n3)
+        l8 = load_list("l8", n8)
+        l7 = load_list("l7", n7)
+
+        warm = keep.tile([P, 2], F32, name="warm")
+        nc.gpsimd.memset(warm[:, 0:1], 1.0)
+        nc.scalar.activation(warm[:, 1:2], warm[:, 0:1], ACT.Abs_reciprocal_sqrt)
+
+        yw = [keep.tile([P, 2 * S], F32, name="yw%d" % t) for t in range(PACK)]
+        for t in range(PACK):
+            nc.vector.memset(tabw[t][:, S:], 0.0)
+        for t in range(PACK):
+            nc.vector.memset(yw[t][:, S:], 0.0)
+
+        banks = [psum.tile([P, S], F32, name="bank%d" % b) for b in range(2 * PACK)]
+
+        w1 = deal("w1", w1w_raw, w1s_raw)
+        x_codes = keep.tile([P, S], U32, name="x_codes", align_bytes=64)
+        x_bytes = keep.tile([P, S], U8, name="x_bytes", align_bytes=64)
+        nc.vector.tensor_copy(x_codes[:], xw[:].indirect(picks[:]))
+        nc.vector.tensor_copy(x_bytes[:], xs[:].indirect(picks[:]))
+        w2 = deal("w2", w2w_raw, w2s_raw)
+
+        for t in range(PACK):
+            nc.scalar.activation(tabw[t][:, :S], tab_raw[t // 2][:, t % 2, :], ACT.Copy, scale=gain[:, t : t + 1])
+        minus_gain = keep.tile([P, PACK], F32, name="minus_gain")
+        nc.scalar.activation(minus_gain[:], gain[:], ACT.Copy, scale=-1.0)
+        factor = keep.tile([P, PACK, S], F32, name="factor")
+        for t in range(PACK):
+            nc.vector.tensor_copy(factor[:, t, :], tabw[t][:].indirect(l4[:]))
+
+        y_plain = keep.tile([P, PACK, S], F32, name="y_plain")
+        for t in range(PACK):
+            product(banks[t][:], w1, t, x_codes[:], x_bytes[:])
+            nc.scalar.copy(yw[t][:, :S], banks[t][:])
+        for t in range(PACK):
+            nc.scalar.copy(y_plain[:, t, :], banks[t][:])
+
+        prod = keep.tile([P, PACK, S], F32, name="prod")
+        z2 = keep.tile([P, PACK, S], F32, name="z2")
+        for t in range(PACK):
+            nc.vector.tensor_tensor(prod[:, t, :], yw[t][:].indirect(l6[:]), factor[:, t, :], ALU.mult)
+        for t in range(PACK):
+            nc.vector.tensor_tensor(z2[:, t, :], tabw[t][:].indirect(l5[:]), prod[:, t, :], ALU.add)
+        z2_bf = keep.tile([P, S, PACK], BF16, name="z2_bf", align_bytes=64)
+        nc.scalar.copy(
+            z2_bf[:].rearrange("p (c i) t -> p c t i", i=4),
+            z2[:].rearrange("p t (c i) -> p c t i", i=4),
+        )
+        z2_codes = keep.tile([P, S], U32, name="z2_codes", align_bytes=64)
+        z2_scales = keep.tile([P, S], U8, name="z2_scales", align_bytes=64)
+        bw = [keep.tile([P, 2 * S], F32, name="bw%d" % t) for t in range(PACK)]
+        aw = [keep.tile([P, S], F32, name="aw%d" % t) for t in range(PACK)]
+        a_plain = keep.tile([P, PACK, S], F32, name="a_plain")
+        recip = keep.tile([P, PACK, S], F32, name="recip")
+
+        def z_gathers(h):
+            first = h * HALF
+            both = keep.tile([P, PACK, HALF], F32, name="both%d" % h)
+            less2 = keep.tile([P, PACK, HALF], F32, name="less2_%d" % h)
+            less3 = keep.tile([P, PACK, HALF], F32, name="less3_%d" % h)
+            larger = keep.tile([P, PACK, HALF], F32, name="larger%d" % h)
+            for t in range(PACK):
+                nc.vector.tensor_tensor(both[:, t, :], yw[t][:].indirect(entries(l1, first, HALF)), y_plain[:, t, first : first + HALF], ALU.add)
+            for t in range(PACK):
+                nc.vector.tensor_tensor(less2[:, t, :], yw[t][:].indirect(entries(l2, first, HALF)), both[:, t, :], ALU.subtract)
+            for t in range(PACK):
+                nc.vector.tensor_tensor(less3[:, t, :], yw[t][:].indirect(entries(l3, first, HALF)), both[:, t, :], ALU.subtract)
+            nc.vector.tensor_tensor(larger[:], less2[:], less3[:], ALU.max)
+            return larger
+
+        def z_round(h, larger):
+            z_rows = keep.tile([P, PACK, HALF], BF16, name="z_rows%d" % h)
+            z_bf = keep.tile([P, HALF, PACK], BF16, name="z_bf%d" % h, align_bytes=64)
+            for t in range(PACK):
+                nc.scalar.activation(z_rows[:, t, :], larger[:, t, :], ACT.Copy, scale=minus_gain[:, t : t + 1])
+            nc.scalar.copy(
+                z_bf[:].rearrange("p (c i) t -> p c t i", i=4),
+                z_rows[:].rearrange("p t (c i) -> p c t i", i=4),
+            )
+            return z_bf
+
+        def a_half(h, z_bf):
+            cols = slice(h * HALF, (h + 1) * HALF)
+            z_codes = keep.tile([P, HALF], U32, name="z_codes%d" % h, align_bytes=64)
+            z_scales = keep.tile([P, HALF], U8, name="z_scales%d" % h, align_bytes=64)
+            nc.vector.quantize_mx(out=z_codes[:].bitcast(FP8X4), scales=z_scales[:], in_=z_bf[:].rearrange("p c t -> p (c t)"))
+            for t in range(PACK):
+                product(banks[t][:, cols], w2, t, z_codes[:], z_scales[:])
+                nc.scalar.copy(aw[t][:, cols], banks[t][:, cols])
+                nc.scalar.copy(a_plain[:, t, cols], banks[t][:, cols])
+
+        def denominators(t):
+            sizes = keep.tile([P, S], F32, name="sizes%d" % t)
+            root = keep.tile([P, S], F32, name="root%d" % t)
+            nc.vector.tensor_tensor(sizes[:], bw[t][:].indirect(l8[:]), bw[(t + 1) % PACK][:, S:], ALU.add)
+            nc.scalar.activation(root[:], sizes[:], ACT.Abs_reciprocal_sqrt, bias=0.5)
+            nc.scalar.activation(recip[:, t, :], root[:], ACT.Square)
+
+        larger0 = z_gathers(0)
+        nc.vector.quantize_mx(out=z2_codes[:].bitcast(FP8X4), scales=z2_scales[:], in_=z2_bf[:].rearrange("p c t -> p (c t)"))
+        for t in range(PACK):
+            product(banks[PACK + t][:], w2, t, z2_codes[:], z2_scales[:])
+            nc.scalar.activation(bw[t][:, :S], banks[PACK + t][:], ACT.Abs)
+            nc.scalar.activation(bw[(t + 1) % PACK][:, S:], banks[PACK + t][:], ACT.Abs)
+        z_bf0 = z_round(0, larger0)
+        larger1 = z_gathers(1)
+        a_half(0, z_bf0)
+        z_bf1 = z_round(1, larger1)
+        denominators(0)
+        denominators(1)
+        a_half(1, z_bf1)
+        denominators(2)
+        denominators(3)
+
+        out_rows = out_0.rearrange("(p t) j -> p t j", t=PACK)
+        out_words = out_1[0].rearrange("p c r -> p (c r)").bitcast(I32)
+        o_codes = keep.tile([P, S], U32, name="o_codes", align_bytes=64)
+        o_scales = keep.tile([P, S], U8, name="o_scales", align_bytes=64)
+        for first, count in ((0, 256), (256, 128), (384, 128)):
+            cols = slice(first, first + count)
+            diff = keep.tile([P, PACK, count], F32, name="diff%d" % first)
+            result = keep.tile([P, PACK, count], F32, name="result%d" % first)
+            rounded = keep.tile([P, count, PACK], BF16, name="rounded%d" % first, align_bytes=64)
+            for t in range(PACK):
+                nc.vector.tensor_tensor(diff[:, t, :], aw[t][:].indirect(entries(l7, first, count)), a_plain[:, t, cols], ALU.subtract)
+            nc.vector.scalar_tensor_tensor(result[:], diff[:], -1.0, recip[:, :, cols], ALU.mult, ALU.mult)
+            nc.sync.dma_start(out_rows[:, :, cols], result[:])
+            nc.scalar.copy(
+                rounded[:].rearrange("p (c i) t -> p c t i", i=4),
+                result[:].rearrange("p t (c i) -> p c t i", i=4),
+            )
+            nc.vector.quantize_mx(out=o_codes[:, cols].bitcast(FP8X4), scales=o_scales[:, cols], in_=rounded[:].rearrange("p c t -> p (c t)"))
+            nc.sync.dma_start(out_words[:, cols], o_codes[:, cols].bitcast(I32))
+        for q in range(4):
+            queue = nc.sync if q % 2 == 0 else nc.scalar
+            queue.dma_start(out_2[0, 4 * q : 4 * q + 4, :].bitcast(I32), o_scales[32 * q : 32 * q + 4, :].bitcast(I32))

@@ -46,14 +46,14 @@ def tile_picked_tienormbtrimkinda_none_po_kernel(
                 queue.dma_start(tile[32 * q : 32 * q + 4, :].bitcast(I32), src[0, 4 * q : 4 * q + 4, :].bitcast(I32))
             return tile
 
-        def deal(name, words_raw, scales_raw):
+        def deal(engine, name, words_raw, scales_raw):
             words = keep.tile([P, 2 * H], U8, name=name + "_words", align_bytes=64)
             scales = keep.tile([P, H], U8, name=name + "_scales", align_bytes=64)
-            nc.vector.tensor_copy(
+            engine.tensor_copy(
                 words[:].rearrange("p (t m b) -> p t m b", t=PACK, b=2),
                 words_raw[:].rearrange("p (m t b) -> p t m b", t=PACK, b=2),
             )
-            nc.vector.tensor_copy(
+            engine.tensor_copy(
                 scales[:].rearrange("p (t m) -> p t m", t=PACK),
                 scales_raw[:].rearrange("p (m t) -> p t m", t=PACK),
             )
@@ -71,28 +71,28 @@ def tile_picked_tienormbtrimkinda_none_po_kernel(
                 stop=True,
             )
 
-        w1s_raw = load_scale_rows(nc.scalar, nc.gpsimd, "w1s_raw", w1_scales, H)
-        xs = load_scale_rows(nc.scalar, nc.gpsimd, "xs", x_scales, T)
-        w2s_raw = load_scale_rows(nc.gpsimd, nc.gpsimd, "w2s_raw", w2_scales, H)
-
         tab_rows = tab.rearrange("(p t) j -> p t j", t=PACK)
-        tab_raw = [keep.tile([P, 2, S], F32, name="tab_raw%d" % u) for u in range(2)]
         tabw = [keep.tile([P, 2 * S], F32, name="tabw%d" % t) for t in range(PACK)]
         gain = keep.tile([P, PACK], F32, name="gain")
         xw = keep.tile([P, T], U32, name="xw")
         w1w_raw = keep.tile([P, 2 * H], U8, name="w1w_raw")
         w2w_raw = keep.tile([P, 2 * H], U8, name="w2w_raw")
 
-        nc.sync.dma_start(w1w_raw[:].bitcast(I32), w1_words[0].bitcast(I32))
-        nc.sync.dma_start(w2w_raw[:].bitcast(I32), w2_words[0].bitcast(I32))
-        nc.sync.dma_start(xw[:].bitcast(I32), x_words[0].rearrange("p c r -> p (c r)").bitcast(I32))
-        picks = load_list("picks", offs)
         nc.sync.dma_start(gain[:], gn.rearrange("(p t) o -> p (t o)", t=PACK))
-        nc.sync.dma_start(tab_raw[0][:], tab_rows[:, 0:2, :])
+        nc.sync.dma_start(tabw[0][:, S:], tab_rows[:, 0, :])
         l4 = load_list("l4", n4)
-        nc.sync.dma_start(tab_raw[1][:], tab_rows[:, 2:4, :])
+        nc.sync.dma_start(tabw[1][:, S:], tab_rows[:, 1, :])
+        nc.sync.dma_start(w1w_raw[:].bitcast(I32), w1_words[0].bitcast(I32))
+        picks = load_list("picks", offs)
+        nc.sync.dma_start(xw[:].bitcast(I32), x_words[0].rearrange("p c r -> p (c r)").bitcast(I32))
+        xs = load_scale_rows(nc.sync, nc.vector, "xs", x_scales, T)
+        w1s_raw = load_scale_rows(nc.sync, nc.vector, "w1s_raw", w1_scales, H)
+        for t in range(2, PACK):
+            nc.sync.dma_start(tabw[t][:, S:], tab_rows[:, t, :])
+        nc.sync.dma_start(w2w_raw[:].bitcast(I32), w2_words[0].bitcast(I32))
         l6 = load_list("l6", n6)
         l5 = load_list("l5", n5)
+        w2s_raw = load_scale_rows(nc.sync, nc.vector, "w2s_raw", w2_scales, H)
         l1 = load_list("l1", n1)
         l2 = load_list("l2", n2)
         l3 = load_list("l3", n3)
@@ -100,38 +100,36 @@ def tile_picked_tienormbtrimkinda_none_po_kernel(
         l7 = load_list("l7", n7)
 
         warm = keep.tile([P, 2], F32, name="warm")
-        nc.gpsimd.memset(warm[:, 0:1], 1.0)
+        nc.vector.memset(warm[:, 0:1], 1.0)
         nc.scalar.activation(warm[:, 1:2], warm[:, 0:1], ACT.Abs_reciprocal_sqrt)
-
-        yw = [keep.tile([P, 2 * S], F32, name="yw%d" % t) for t in range(PACK)]
-        for t in range(PACK):
-            nc.vector.memset(tabw[t][:, S:], 0.0)
-        for t in range(PACK):
-            nc.vector.memset(yw[t][:, S:], 0.0)
 
         banks = [psum.tile([P, S], F32, name="bank%d" % b) for b in range(2 * PACK)]
 
-        w1 = deal("w1", w1w_raw, w1s_raw)
+        for t in range(PACK):
+            nc.scalar.activation(tabw[t][:, :S], tabw[t][:, S:], ACT.Copy, scale=gain[:, t : t + 1])
+        minus_gain = keep.tile([P, PACK], F32, name="minus_gain")
+        nc.scalar.activation(minus_gain[:], gain[:], ACT.Copy, scale=-1.0)
+        factor = keep.tile([P, PACK, S], F32, name="factor")
+        for t in range(2):
+            nc.vector.tensor_copy(factor[:, t, :], tabw[t][:].indirect(l4[:]))
+        w1 = deal(nc.vector, "w1", w1w_raw, w1s_raw)
         x_codes = keep.tile([P, S], U32, name="x_codes", align_bytes=64)
         x_bytes = keep.tile([P, S], U8, name="x_bytes", align_bytes=64)
         nc.vector.tensor_copy(x_codes[:], xw[:].indirect(picks[:]))
         nc.vector.tensor_copy(x_bytes[:], xs[:].indirect(picks[:]))
-        w2 = deal("w2", w2w_raw, w2s_raw)
-
-        for t in range(PACK):
-            nc.scalar.activation(tabw[t][:, :S], tab_raw[t // 2][:, t % 2, :], ACT.Copy, scale=gain[:, t : t + 1])
-        minus_gain = keep.tile([P, PACK], F32, name="minus_gain")
-        nc.scalar.activation(minus_gain[:], gain[:], ACT.Copy, scale=-1.0)
-        factor = keep.tile([P, PACK, S], F32, name="factor")
-        for t in range(PACK):
+        for t in range(2, PACK):
             nc.vector.tensor_copy(factor[:, t, :], tabw[t][:].indirect(l4[:]))
+        w2 = deal(nc.vector, "w2", w2w_raw, w2s_raw)
 
-        y_plain = keep.tile([P, PACK, S], F32, name="y_plain")
+        yw = [keep.tile([P, 2 * S], F32, name="yw%d" % t) for t in range(PACK)]
         for t in range(PACK):
             product(banks[t][:], w1, t, x_codes[:], x_bytes[:])
-            nc.scalar.copy(yw[t][:, :S], banks[t][:])
         for t in range(PACK):
-            nc.scalar.copy(y_plain[:, t, :], banks[t][:])
+            nc.scalar.copy(yw[t][:, :S], banks[t][:])
+            nc.scalar.copy(yw[t][:, S:], banks[(t + 1) % PACK][:])
+
+        def y_plain(t, first, count):
+            return yw[(t - 1) % PACK][:, S + first : S + first + count]
 
         prod = keep.tile([P, PACK, S], F32, name="prod")
         z2 = keep.tile([P, PACK, S], F32, name="z2")
@@ -139,82 +137,96 @@ def tile_picked_tienormbtrimkinda_none_po_kernel(
             nc.vector.tensor_tensor(prod[:, t, :], yw[t][:].indirect(l6[:]), factor[:, t, :], ALU.mult)
         for t in range(PACK):
             nc.vector.tensor_tensor(z2[:, t, :], tabw[t][:].indirect(l5[:]), prod[:, t, :], ALU.add)
-        z2_bf = keep.tile([P, S, PACK], BF16, name="z2_bf", align_bytes=64)
-        nc.scalar.copy(
-            z2_bf[:].rearrange("p (c i) t -> p c t i", i=4),
-            z2[:].rearrange("p t (c i) -> p c t i", i=4),
-        )
-        z2_codes = keep.tile([P, S], U32, name="z2_codes", align_bytes=64)
-        z2_scales = keep.tile([P, S], U8, name="z2_scales", align_bytes=64)
-        bw = [keep.tile([P, 2 * S], F32, name="bw%d" % t) for t in range(PACK)]
+
+        def interleave(engine_copy, dst, src):
+            engine_copy(dst.rearrange("p (c i) t -> p c t i", i=4), src.rearrange("p t (c i) -> p c t i", i=4))
+
+        def quantize(codes, scales, rounded):
+            nc.vector.quantize_mx(out=codes.bitcast(FP8X4), scales=scales, in_=rounded.rearrange("p c t -> p (c t)"))
+
+        def gather_y(out, places, first, other, op):
+            for t in range(PACK):
+                nc.vector.tensor_tensor(out[:, t, :], yw[t][:].indirect(entries(places, first, HALF)), other(t), op)
+
+        def z_start(h):
+            first = h * HALF
+            both = keep.tile([P, PACK, HALF], F32, name="both")
+            less2 = keep.tile([P, PACK, HALF], F32, name="less2", tag="ring_b")
+            gather_y(both, l1, first, lambda t: y_plain(t, first, HALF), ALU.add)
+            gather_y(less2, l2, first, lambda t: both[:, t, :], ALU.subtract)
+            return both, less2
+
+        def z_finish(h, both, less2):
+            less3 = keep.tile([P, PACK, HALF], F32, name="less3", tag="ring_a", align_bytes=64)
+            larger = keep.tile([P, PACK, HALF], F32, name="larger")
+            gather_y(less3, l3, h * HALF, lambda t: both[:, t, :], ALU.subtract)
+            nc.vector.tensor_tensor(larger[:], less2[:], less3[:], ALU.max)
+            z_rows = keep.tile([P, PACK, HALF], BF16, name="z_rows", tag="ring_c")
+            z_bf = keep.tile([P, HALF, PACK], BF16, name="z_bf", tag="ring_a", align_bytes=64)
+            for t in range(PACK):
+                nc.scalar.activation(z_rows[:, t, :], larger[:, t, :], ACT.Copy, scale=minus_gain[:, t : t + 1])
+            interleave(nc.scalar.copy, z_bf[:], z_rows[:])
+            return z_bf
+
         aw = [keep.tile([P, S], F32, name="aw%d" % t) for t in range(PACK)]
         a_plain = keep.tile([P, PACK, S], F32, name="a_plain")
         recip = keep.tile([P, PACK, S], F32, name="recip")
+        bw = [keep.tile([P, 2 * S], F32, name="bw%d" % t) for t in range(PACK)]
 
-        def z_gathers(h):
-            first = h * HALF
-            both = keep.tile([P, PACK, HALF], F32, name="both%d" % h)
-            less2 = keep.tile([P, PACK, HALF], F32, name="less2_%d" % h)
-            less3 = keep.tile([P, PACK, HALF], F32, name="less3_%d" % h)
-            larger = keep.tile([P, PACK, HALF], F32, name="larger%d" % h)
-            for t in range(PACK):
-                nc.vector.tensor_tensor(both[:, t, :], yw[t][:].indirect(entries(l1, first, HALF)), y_plain[:, t, first : first + HALF], ALU.add)
-            for t in range(PACK):
-                nc.vector.tensor_tensor(less2[:, t, :], yw[t][:].indirect(entries(l2, first, HALF)), both[:, t, :], ALU.subtract)
-            for t in range(PACK):
-                nc.vector.tensor_tensor(less3[:, t, :], yw[t][:].indirect(entries(l3, first, HALF)), both[:, t, :], ALU.subtract)
-            nc.vector.tensor_tensor(larger[:], less2[:], less3[:], ALU.max)
-            return larger
-
-        def z_round(h, larger):
-            z_rows = keep.tile([P, PACK, HALF], BF16, name="z_rows%d" % h)
-            z_bf = keep.tile([P, HALF, PACK], BF16, name="z_bf%d" % h, align_bytes=64)
-            for t in range(PACK):
-                nc.scalar.activation(z_rows[:, t, :], larger[:, t, :], ACT.Copy, scale=minus_gain[:, t : t + 1])
-            nc.scalar.copy(
-                z_bf[:].rearrange("p (c i) t -> p c t i", i=4),
-                z_rows[:].rearrange("p t (c i) -> p c t i", i=4),
-            )
-            return z_bf
-
-        def a_half(h, z_bf):
+        def a_products(h, z_bf):
             cols = slice(h * HALF, (h + 1) * HALF)
             z_codes = keep.tile([P, HALF], U32, name="z_codes%d" % h, align_bytes=64)
             z_scales = keep.tile([P, HALF], U8, name="z_scales%d" % h, align_bytes=64)
-            nc.vector.quantize_mx(out=z_codes[:].bitcast(FP8X4), scales=z_scales[:], in_=z_bf[:].rearrange("p c t -> p (c t)"))
+            quantize(z_codes[:], z_scales[:], z_bf[:])
             for t in range(PACK):
                 product(banks[t][:, cols], w2, t, z_codes[:], z_scales[:])
-                nc.scalar.copy(aw[t][:, cols], banks[t][:, cols])
-                nc.scalar.copy(a_plain[:, t, cols], banks[t][:, cols])
 
-        def denominators(t):
-            sizes = keep.tile([P, S], F32, name="sizes%d" % t)
-            root = keep.tile([P, S], F32, name="root%d" % t)
-            nc.vector.tensor_tensor(sizes[:], bw[t][:].indirect(l8[:]), bw[(t + 1) % PACK][:, S:], ALU.add)
+        def a_out(h, target):
+            cols = slice(h * HALF, (h + 1) * HALF)
+            for t in range(PACK):
+                nc.scalar.copy(target(t)[:, cols], banks[t][:, cols])
+
+        def b_sizes(pair, sizes):
+            for u in range(2):
+                t = 2 * pair + u
+                nc.vector.tensor_tensor(sizes[:, u, :], bw[t][:].indirect(l8[:]), bw[(t + 1) % PACK][:, S:], ALU.add)
+
+        def reciprocals(pair, sizes):
+            root = keep.tile([P, 2, S], F32, name="root", tag="ring_c")
             nc.scalar.activation(root[:], sizes[:], ACT.Abs_reciprocal_sqrt, bias=0.5)
-            nc.scalar.activation(recip[:, t, :], root[:], ACT.Square)
+            nc.scalar.activation(recip[:, 2 * pair : 2 * pair + 2, :], root[:], ACT.Square)
 
-        larger0 = z_gathers(0)
-        nc.vector.quantize_mx(out=z2_codes[:].bitcast(FP8X4), scales=z2_scales[:], in_=z2_bf[:].rearrange("p c t -> p (c t)"))
+        z2_bf = keep.tile([P, S, PACK], BF16, name="z2_bf", tag="ring_a", align_bytes=64)
+        interleave(nc.scalar.copy, z2_bf[:], z2[:])
+        both, less2 = z_start(0)
+        z2_codes = keep.tile([P, S], U32, name="z2_codes", align_bytes=64)
+        z2_scales = keep.tile([P, S], U8, name="z2_scales", align_bytes=64)
+        quantize(z2_codes[:], z2_scales[:], z2_bf[:])
         for t in range(PACK):
             product(banks[PACK + t][:], w2, t, z2_codes[:], z2_scales[:])
             nc.scalar.activation(bw[t][:, :S], banks[PACK + t][:], ACT.Abs)
             nc.scalar.activation(bw[(t + 1) % PACK][:, S:], banks[PACK + t][:], ACT.Abs)
-        z_bf0 = z_round(0, larger0)
-        larger1 = z_gathers(1)
-        a_half(0, z_bf0)
-        z_bf1 = z_round(1, larger1)
-        denominators(0)
-        denominators(1)
-        a_half(1, z_bf1)
-        denominators(2)
-        denominators(3)
+        z_bf = z_finish(0, both, less2)
+        both, less2 = z_start(1)
+        a_products(0, z_bf)
+        a_out(0, lambda t: aw[t])
+        a_out(0, lambda t: a_plain[:, t, :])
+        z_bf = z_finish(1, both, less2)
+        sizes0 = keep.tile([P, 2, S], F32, name="sizes0", tag="ring_b")
+        b_sizes(0, sizes0)
+        a_products(1, z_bf)
+        sizes1 = keep.tile([P, 2, S], F32, name="sizes1", tag="ring_a", align_bytes=64)
+        b_sizes(1, sizes1)
+        reciprocals(0, sizes0)
+        a_out(1, lambda t: aw[t])
+        reciprocals(1, sizes1)
+        a_out(1, lambda t: a_plain[:, t, :])
 
         out_rows = out_0.rearrange("(p t) j -> p t j", t=PACK)
         out_words = out_1[0].rearrange("p c r -> p (c r)").bitcast(I32)
         o_codes = keep.tile([P, S], U32, name="o_codes", align_bytes=64)
         o_scales = keep.tile([P, S], U8, name="o_scales", align_bytes=64)
-        for first, count in ((0, 256), (256, 128), (384, 128)):
+        for first, count, rounder in ((0, 256, nc.scalar.copy), (256, 128, nc.scalar.copy), (384, 128, nc.vector.tensor_copy)):
             cols = slice(first, first + count)
             diff = keep.tile([P, PACK, count], F32, name="diff%d" % first)
             result = keep.tile([P, PACK, count], F32, name="result%d" % first)
@@ -223,11 +235,8 @@ def tile_picked_tienormbtrimkinda_none_po_kernel(
                 nc.vector.tensor_tensor(diff[:, t, :], aw[t][:].indirect(entries(l7, first, count)), a_plain[:, t, cols], ALU.subtract)
             nc.vector.scalar_tensor_tensor(result[:], diff[:], -1.0, recip[:, :, cols], ALU.mult, ALU.mult)
             nc.sync.dma_start(out_rows[:, :, cols], result[:])
-            nc.scalar.copy(
-                rounded[:].rearrange("p (c i) t -> p c t i", i=4),
-                result[:].rearrange("p t (c i) -> p c t i", i=4),
-            )
-            nc.vector.quantize_mx(out=o_codes[:, cols].bitcast(FP8X4), scales=o_scales[:, cols], in_=rounded[:].rearrange("p c t -> p (c t)"))
+            interleave(rounder, rounded[:], result[:])
+            quantize(o_codes[:, cols], o_scales[:, cols], rounded[:])
             nc.sync.dma_start(out_words[:, cols], o_codes[:, cols].bitcast(I32))
         for q in range(4):
             queue = nc.sync if q % 2 == 0 else nc.scalar

@@ -78,18 +78,18 @@ def tile_picked_tienormbtrimkinda_none_po_kernel(
         w1w_raw = keep.tile([P, 2 * H], U8, name="w1w_raw")
         w2w_raw = keep.tile([P, 2 * H], U8, name="w2w_raw")
 
+        nc.sync.dma_start(w1w_raw[:].bitcast(I32), w1_words[0].bitcast(I32))
         nc.sync.dma_start(gain[:], gn.rearrange("(p t) o -> p (t o)", t=PACK))
         nc.sync.dma_start(tabw[0][:, S:], tab_rows[:, 0, :])
         l4 = load_list("l4", n4)
+        nc.sync.dma_start(w2w_raw[:].bitcast(I32), w2_words[0].bitcast(I32))
         nc.sync.dma_start(tabw[1][:, S:], tab_rows[:, 1, :])
-        nc.sync.dma_start(w1w_raw[:].bitcast(I32), w1_words[0].bitcast(I32))
         picks = load_list("picks", offs)
         nc.sync.dma_start(xw[:].bitcast(I32), x_words[0].rearrange("p c r -> p (c r)").bitcast(I32))
         xs = load_scale_rows(nc.sync, nc.vector, "xs", x_scales, T)
         w1s_raw = load_scale_rows(nc.sync, nc.vector, "w1s_raw", w1_scales, H)
         for t in range(2, PACK):
             nc.sync.dma_start(tabw[t][:, S:], tab_rows[:, t, :])
-        nc.sync.dma_start(w2w_raw[:].bitcast(I32), w2_words[0].bitcast(I32))
         l6 = load_list("l6", n6)
         l5 = load_list("l5", n5)
         w2s_raw = load_scale_rows(nc.sync, nc.vector, "w2s_raw", w2_scales, H)
@@ -191,10 +191,11 @@ def tile_picked_tienormbtrimkinda_none_po_kernel(
                 t = 2 * pair + u
                 nc.vector.tensor_tensor(sizes[:, u, :], bw[t][:].indirect(l8[:]), bw[(t + 1) % PACK][:, S:], ALU.add)
 
-        def reciprocals(pair, sizes):
-            root = keep.tile([P, 2, S], F32, name="root", tag="ring_c")
-            nc.scalar.activation(root[:], sizes[:], ACT.Abs_reciprocal_sqrt, bias=0.5)
-            nc.scalar.activation(recip[:, 2 * pair : 2 * pair + 2, :], root[:], ACT.Square)
+        def reciprocals(pair, sizes, first, count):
+            cols = slice(first, first + count)
+            root = keep.tile([P, 2, count], F32, name="root", tag="ring_c")
+            nc.scalar.activation(root[:], sizes[:, :, cols], ACT.Abs_reciprocal_sqrt, bias=0.5)
+            nc.scalar.activation(recip[:, 2 * pair : 2 * pair + 2, cols], root[:], ACT.Square)
 
         z2_bf = keep.tile([P, S, PACK], BF16, name="z2_bf", tag="ring_a", align_bytes=64)
         interleave(nc.scalar.copy, z2_bf[:], z2[:])
@@ -217,10 +218,11 @@ def tile_picked_tienormbtrimkinda_none_po_kernel(
         a_products(1, z_bf)
         sizes1 = keep.tile([P, 2, S], F32, name="sizes1", tag="ring_a", align_bytes=64)
         b_sizes(1, sizes1)
-        reciprocals(0, sizes0)
+        reciprocals(0, sizes0, 0, S)
         a_out(1, lambda t: aw[t])
-        reciprocals(1, sizes1)
+        reciprocals(1, sizes1, 0, HALF)
         a_out(1, lambda t: a_plain[:, t, :])
+        reciprocals(1, sizes1, HALF, HALF)
 
         out_rows = out_0.rearrange("(p t) j -> p t j", t=PACK)
         out_words = out_1[0].rearrange("p c r -> p (c r)").bitcast(I32)

from contextlib import ExitStack

import concourse.mybir as mybir

K, T, S, H = 512, 2048, 512, 512
FLOPS = 3 * 2 * K * H * S

F32 = mybir.dt.float32
BF16 = mybir.dt.bfloat16
I32 = mybir.dt.int32
U32 = mybir.dt.uint32
U16 = mybir.dt.uint16
U8 = mybir.dt.uint8
FP8X4 = mybir.dt.float8_e4m3fn_x4
FP4X4 = mybir.dt.float4_e2m1fn_x4
ALU = mybir.AluOpType
ACT = mybir.ActivationFunctionType

P = 128
PACK = 4
HALF = S // 2
LANES = 16


def tile_picked_tienormbtrimkinda_none_po_kernel(
    tc, x_words, x_scales, w1_words, w1_scales, tab, gn, w2_words, w2_scales,
    offs, n1, n2, n3, n4, n5, n6, n7, n8, out_0, out_1, out_2,
):
    nc = tc.nc
    with ExitStack() as ctx:
        keep = ctx.enter_context(tc.tile_pool(name="keep", bufs=1))
        psum = ctx.enter_context(tc.psum_pool(name="psum", bufs=1))

        def load_list(name, src):
            tile = keep.tile([P, S // LANES], U16, name=name)
            nc.sync.dma_start(tile[:], src)
            return tile

        def entries(tile, first, count):
            return tile[:, first // LANES : (first + count) // LANES]

        def load_scale_rows(queue, clear, name, src, width):
            tile = keep.tile([P, width], U8, name=name, align_bytes=64)
            clear.memset(tile[:].bitcast(I32), 0)
            for q in range(4):
                queue.dma_start(tile[32 * q : 32 * q + 4, :].bitcast(I32), src[0, 4 * q : 4 * q + 4, :].bitcast(I32))
            return tile

        def deal(engine, name, words_raw, scales_raw):
            words = keep.tile([P, 2 * H], U8, name=name + "_words", align_bytes=64)
            scales = keep.tile([P, H], U8, name=name + "_scales", align_bytes=64)
            engine.tensor_copy(
                words[:].rearrange("p (t m b) -> p t m b", t=PACK, b=2),
                words_raw[:].rearrange("p (m t b) -> p t m b", t=PACK, b=2),
            )
            engine.tensor_copy(
                scales[:].rearrange("p (t m) -> p t m", t=PACK),
                scales_raw[:].rearrange("p (m t) -> p t m", t=PACK),
            )
            return words, scales

        def product(out, weights, t, codes, scales):
            words, w_scales = weights
            nc.tensor.matmul_mx(
                out=out,
                lhsT=words[:, 2 * P * t : 2 * P * (t + 1)].bitcast(FP4X4),
                lhsT_scale=w_scales[:, P * t : P * (t + 1)],
                rhs=codes.bitcast(FP8X4),
                rhs_scale=scales,
                start=True,
                stop=True,
            )

        tab_rows = tab.rearrange("(p t) j -> p t j", t=PACK)
        tabw = [keep.tile([P, 2 * S], F32, name="tabw%d" % t) for t in range(PACK)]
        gain = keep.tile([P, PACK], F32, name="gain")
        xw = keep.tile([P, T], U32, name="xw")
        w1w_raw = keep.tile([P, 2 * H], U8, name="w1w_raw")
        w2w_raw = keep.tile([P, 2 * H], U8, name="w2w_raw")

        nc.sync.dma_start(w1w_raw[:].bitcast(I32), w1_words[0].bitcast(I32))
        nc.sync.dma_start(gain[:], gn.rearrange("(p t) o -> p (t o)", t=PACK))
        nc.sync.dma_start(tabw[0][:, S:], tab_rows[:, 0, :])
        l4 = load_list("l4", n4)
        nc.sync.dma_start(w2w_raw[:].bitcast(I32), w2_words[0].bitcast(I32))
        nc.sync.dma_start(tabw[1][:, S:], tab_rows[:, 1, :])
        picks = load_list("picks", offs)
        nc.sync.dma_start(xw[:].bitcast(I32), x_words[0].rearrange("p c r -> p (c r)").bitcast(I32))
        xs = load_scale_rows(nc.sync, nc.vector, "xs", x_scales, T)
        w1s_raw = load_scale_rows(nc.sync, nc.vector, "w1s_raw", w1_scales, H)
        for t in range(2, PACK):
            nc.sync.dma_start(tabw[t][:, S:], tab_rows[:, t, :])
        l6 = load_list("l6", n6)
        l5 = load_list("l5", n5)
        w2s_raw = load_scale_rows(nc.sync, nc.vector, "w2s_raw", w2_scales, H)
        l1 = load_list("l1", n1)
        l2 = load_list("l2", n2)
        l3 = load_list("l3", n3)
        l8 = load_list("l8", n8)
        l7 = load_list("l7", n7)

        warm = keep.tile([P, 2], F32, name="warm")
        nc.vector.memset(warm[:, 0:1], 1.0)
        nc.scalar.activation(warm[:, 1:2], warm[:, 0:1], ACT.Abs_reciprocal_sqrt)

        banks = [psum.tile([P, S], F32, name="bank%d" % b) for b in range(2 * PACK)]

        for t in range(PACK):
            nc.scalar.activation(tabw[t][:, :S], tabw[t][:, S:], ACT.Copy, scale=gain[:, t : t + 1])
        minus_gain = keep.tile([P, PACK], F32, name="minus_gain")
        nc.scalar.activation(minus_gain[:], gain[:], ACT.Copy, scale=-1.0)
        factor = keep.tile([P, PACK, S], F32, name="factor")
        for t in range(2):
            nc.vector.tensor_copy(factor[:, t, :], tabw[t][:].indirect(l4[:]))
        w1 = deal(nc.vector, "w1", w1w_raw, w1s_raw)
        x_codes = keep.tile([P, S], U32, name="x_codes", align_bytes=64)
        x_bytes = keep.tile([P, S], U8, name="x_bytes", align_bytes=64)
        nc.vector.tensor_copy(x_codes[:], xw[:].indirect(picks[:]))
        nc.vector.tensor_copy(x_bytes[:], xs[:].indirect(picks[:]))
        for t in range(2, PACK):
            nc.vector.tensor_copy(factor[:, t, :], tabw[t][:].indirect(l4[:]))
        w2 = deal(nc.vector, "w2", w2w_raw, w2s_raw)

        yw = [keep.tile([P, 2 * S], F32, name="yw%d" % t) for t in range(PACK)]
        for t in range(PACK):
            product(banks[t][:], w1, t, x_codes[:], x_bytes[:])
        for t in range(PACK):
            nc.scalar.copy(yw[t][:, :S], banks[t][:])
            nc.scalar.copy(yw[t][:, S:], banks[(t + 1) % PACK][:])

        def y_plain(t, first, count):
            return yw[(t - 1) % PACK][:, S + first : S + first + count]

        prod = keep.tile([P, PACK, S], F32, name="prod")
        z2 = keep.tile([P, PACK, S], F32, name="z2")
        for t in range(PACK):
            nc.vector.tensor_tensor(prod[:, t, :], yw[t][:].indirect(l6[:]), factor[:, t, :], ALU.mult)
        for t in range(PACK):
            nc.vector.tensor_tensor(z2[:, t, :], tabw[t][:].indirect(l5[:]), prod[:, t, :], ALU.add)

        def interleave(engine_copy, dst, src):
            engine_copy(dst.rearrange("p (c i) t -> p c t i", i=4), src.rearrange("p t (c i) -> p c t i", i=4))

        def quantize(codes, scales, rounded):
            nc.vector.quantize_mx(out=codes.bitcast(FP8X4), scales=scales, in_=rounded.rearrange("p c t -> p (c t)"))

        def gather_y(out, places, first, other, op):
            for t in range(PACK):
                nc.vector.tensor_tensor(out[:, t, :], yw[t][:].indirect(entries(places, first, HALF)), other(t), op)

        def z_start(h):
            first = h * HALF
            both = keep.tile([P, PACK, HALF], F32, name="both")
            less2 = keep.tile([P, PACK, HALF], F32, name="less2", tag="ring_b")
            gather_y(both, l1, first, lambda t: y_plain(t, first, HALF), ALU.add)
            gather_y(less2, l2, first, lambda t: both[:, t, :], ALU.subtract)
            return both, less2

        def z_finish(h, both, less2):
            less3 = keep.tile([P, PACK, HALF], F32, name="less3", tag="ring_a", align_bytes=64)
            larger = keep.tile([P, PACK, HALF], F32, name="larger")
            gather_y(less3, l3, h * HALF, lambda t: both[:, t, :], ALU.subtract)
            nc.vector.tensor_tensor(larger[:], less2[:], less3[:], ALU.max)
            z_rows = keep.tile([P, PACK, HALF], BF16, name="z_rows", tag="ring_c")
            z_bf = keep.tile([P, HALF, PACK], BF16, name="z_bf", tag="ring_a", align_bytes=64)
            for t in range(PACK):
                nc.scalar.activation(z_rows[:, t, :], larger[:, t, :], ACT.Copy, scale=minus_gain[:, t : t + 1])
            interleave(nc.scalar.copy, z_bf[:], z_rows[:])
            return z_bf

        aw = [keep.tile([P, S], F32, name="aw%d" % t) for t in range(PACK)]
        a_plain = keep.tile([P, PACK, S], F32, name="a_plain")
        recip = keep.tile([P, PACK, S], F32, name="recip")
        bw = [keep.tile([P, 2 * S], F32, name="bw%d" % t) for t in range(PACK)]

        def a_products(h, z_bf):
            cols = slice(h * HALF, (h + 1) * HALF)
            z_codes = keep.tile([P, HALF], U32, name="z_codes%d" % h, align_bytes=64)
            z_scales = keep.tile([P, HALF], U8, name="z_scales%d" % h, align_bytes=64)
            quantize(z_codes[:], z_scales[:], z_bf[:])
            for t in range(PACK):
                product(banks[t][:, cols], w2, t, z_codes[:], z_scales[:])

        def a_out(h, target):
            cols = slice(h * HALF, (h + 1) * HALF)
            for t in range(PACK):
                nc.scalar.copy(target(t)[:, cols], banks[t][:, cols])

        def b_sizes(pair, sizes):
            for u in range(2):
                t = 2 * pair + u
                nc.vector.tensor_tensor(sizes[:, u, :], bw[t][:].indirect(l8[:]), bw[(t + 1) % PACK][:, S:], ALU.add)

        def reciprocals(pair, sizes, first, count):
            cols = slice(first, first + count)
            root = keep.tile([P, 2, count], F32, name="root", tag="ring_c")
            nc.scalar.activation(root[:], sizes[:, :, cols], ACT.Abs_reciprocal_sqrt, bias=0.5)
            nc.scalar.activation(recip[:, 2 * pair : 2 * pair + 2, cols], root[:], ACT.Square)

        z2_bf = keep.tile([P, S, PACK], BF16, name="z2_bf", tag="ring_a", align_bytes=64)
        interleave(nc.scalar.copy, z2_bf[:], z2[:])
        both, less2 = z_start(0)
        z2_codes = keep.tile([P, S], U32, name="z2_codes", align_bytes=64)
        z2_scales = keep.tile([P, S], U8, name="z2_scales", align_bytes=64)
        quantize(z2_codes[:], z2_scales[:], z2_bf[:])
        for t in range(PACK):
            product(banks[PACK + t][:], w2, t, z2_codes[:], z2_scales[:])
            nc.scalar.activation(bw[t][:, :S], banks[PACK + t][:], ACT.Abs)
            nc.scalar.activation(bw[(t + 1) % PACK][:, S:], banks[PACK + t][:], ACT.Abs)
        z_bf = z_finish(0, both, less2)
        both, less2 = z_start(1)
        a_products(0, z_bf)
        a_out(0, lambda t: aw[t])
        a_out(0, lambda t: a_plain[:, t, :])
        z_bf = z_finish(1, both, less2)
        sizes0 = keep.tile([P, 2, S], F32, name="sizes0", tag="ring_b")
        b_sizes(0, sizes0)
        a_products(1, z_bf)
        sizes1 = keep.tile([P, 2, S], F32, name="sizes1", tag="ring_a", align_bytes=64)
        b_sizes(1, sizes1)
        reciprocals(0, sizes0, 0, S)
        a_out(1, lambda t: aw[t])
        reciprocals(1, sizes1, 0, HALF)
        a_out(1, lambda t: a_plain[:, t, :])
        reciprocals(1, sizes1, HALF, HALF)

        out_rows = out_0.rearrange("(p t) j -> p t j", t=PACK)
        out_words = out_1[0].rearrange("p c r -> p (c r)").bitcast(I32)
        o_codes = keep.tile([P, S], U32, name="o_codes", align_bytes=64)
        o_scales = keep.tile([P, S], U8, name="o_scales", align_bytes=64)
        for first, count, rounder in ((0, 256, nc.scalar.copy), (256, 128, nc.scalar.copy), (384, 128, nc.vector.tensor_copy)):
            cols = slice(first, first + count)
            diff = keep.tile([P, PACK, count], F32, name="diff%d" % first)
            result = keep.tile([P, PACK, count], F32, name="result%d" % first)
            rounded = keep.tile([P, count, PACK], BF16, name="rounded%d" % first, align_bytes=64)
            for t in range(PACK):
                nc.vector.tensor_tensor(diff[:, t, :], aw[t][:].indirect(entries(l7, first, count)), a_plain[:, t, cols], ALU.subtract)
            nc.vector.scalar_tensor_tensor(result[:], diff[:], -1.0, recip[:, :, cols], ALU.mult, ALU.mult)
            nc.sync.dma_start(out_rows[:, :, cols], result[:])
            interleave(rounder, rounded[:], result[:])
            quantize(o_codes[:, cols], o_scales[:, cols], rounded[:])
            nc.sync.dma_start(out_words[:, cols], o_codes[:, cols].bitcast(I32))
        for q in range(4):
            queue = nc.sync if q % 2 == 0 else nc.scalar
            queue.dma_start(out_2[0, 4 * q : 4 * q + 4, :].bitcast(I32), o_scales[32 * q : 32 * q + 4, :].bitcast(I32))
